import numpy as np
import ml_dtypes


def mxq(x, axis, fmt="e4m3"):
    dtype, down = {"e4m3": (ml_dtypes.float8_e4m3fn, 7), "e5m2": (ml_dtypes.float8_e5m2, 14)}[fmt]
    v = np.moveaxis(np.asarray(x, np.float32).astype(ml_dtypes.bfloat16).astype(np.float64), axis, -1)
    blocks = v.reshape(v.shape[:-1] + (-1, 32))
    amax = np.abs(blocks).max(-1, keepdims=True)
    byte = np.maximum(np.where(amax > 0, np.frexp(amax)[1] - 1 + 127, 0) - down, 1)
    scale = np.exp2(byte - 127.0)
    codes = (blocks / scale).astype(np.float32).astype(dtype).astype(np.float64)
    return np.moveaxis((codes * scale).reshape(v.shape), -1, axis)


WIDE = False


def mx_kscale(k):
    if not WIDE:
        return np.ones(k)
    levels = np.array([10, -10, 5, -5, 0])
    if k % 512:
        return np.exp2(np.random.permutation(np.resize(levels, k // 32))).repeat(32)
    a = np.empty((k // 512, 16))
    for p in range(k // 512):
        a[p, :8] = np.random.permutation(np.resize(levels, 8))
        for g in range(8):
            far = levels[np.abs(levels - a[p, g]) >= 10]
            a[p, g + 8] = far[np.random.randint(len(far))]
    return np.exp2(a.ravel()).repeat(32)


def f64(x):
    return np.asarray(x).astype(np.float64)


def striped(idx):
    return np.tile(idx.reshape(-1, 16).T, (8, 1)).astype(np.uint16)


def unstriped(offs):
    return offs[:16].T.reshape(-1).astype(np.int64)


def relu(v):
    return np.maximum(v, 0.0)


K, T, E, C, N = 2048, 1024, 4, 128, 256


def by_expert(wq, xq):
    return np.concatenate([wq[e].T @ xq[:, e * C:(e + 1) * C] for e in range(E)], axis=1)


def setup_inputs():
    n = np.random.standard_normal
    s = mx_kscale(K)[:, None]
    return {
        "xT": (n((K, T)) * s).astype(np.float32),
        "w": (n((E, K, N)) / np.sqrt(K) / s[None]).astype(np.float32),
        "b": (0.3 * n((N, E))).astype(np.float32),
        "gate": np.tile(np.random.uniform(0.2, 1.0, E * C), (N, 1)).astype(np.float32),
        "offs": striped(np.random.permutation(T)[:E * C]),
    }


def reference(xT, w, b, gate, offs):
    idx = unstriped(offs)
    xq = mxq(f64(xT)[:, idx], 0, "e4m3")
    y = by_expert(mxq(f64(w), 1, "e4m3"), xq)
    y = relu(y + np.repeat(f64(b), C, axis=1))
    out = np.zeros((N, T))
    out[:, idx] = f64(gate) * y
    return out

@@ -1,0 +1,199 @@
+from contextlib import ExitStack
+
+import concourse.mybir as mybir
+
+K, T, E, C, N = 2048, 1024, 4, 128, 256
+FLOPS = 2 * K * N * E * C
+
+F32 = mybir.dt.float32
+BF16 = mybir.dt.bfloat16
+U32 = mybir.dt.uint32
+U16 = mybir.dt.uint16
+U8 = mybir.dt.uint8
+FP8X4 = mybir.dt.float8_e4m3fn_x4
+MULT = mybir.AluOpType.mult
+RELU = mybir.ActivationFunctionType.Relu
+
+P = 128
+PACK = 4
+PASSES = K // (P * PACK)
+CHUNKS = E * PASSES
+HALF = 256
+HALVES = E * C // HALF
+BLOCKS = N // P
+
+W_ON_VECTOR = (6, 10, 14)
+EARLY = 3
+LOADS = (
+    ("x", 0, 5), ("w", 0, 1), ("x", 5, 4), ("w", 1, 1), ("x", 9, 5), ("w", 2, 1), ("x", 14, 2),
+    ("w", 3, 1), ("w", 4, 2), ("gate", 0, 0), ("w", 6, 2), ("w", 8, 2), ("w", 10, 2), ("w", 12, 2),
+    ("w", 14, 1), ("w", 15, 1),
+)
+
+
+def tile_routed_moe_kernel(tc, xT, w, b, gate, offs, out):
+    nc = tc.nc
+    with ExitStack() as ctx:
+        keep = ctx.enter_context(tc.tile_pool(name="keep", bufs=1))
+        g4_pool = ctx.enter_context(tc.tile_pool(name="g4_pool", bufs=4))
+        xg_pool = ctx.enter_context(tc.tile_pool(name="xg_pool", bufs=4))
+        wg_pool = ctx.enter_context(tc.tile_pool(name="wg_pool", bufs=6))
+        psum = ctx.enter_context(tc.psum_pool(name="psum", bufs=1))
+
+        offsets = keep.tile([P, E * C // 16], U16, name="offsets")
+        nc.sync.dma_start(offsets[:], offs)
+        bias = keep.tile([P, BLOCKS, E], F32, name="bias")
+        nc.sync.dma_start(bias[:], b.rearrange("(h p) e -> p h e", p=P))
+
+        x_view = xT.rearrange("(g p t) n -> g p t n", p=P, t=PACK)
+        w_view = w.rearrange("e (g p j) n -> e p g j n", p=P, j=PACK)
+        planes = {}
+        w_raw = {}
+        gate_sb = keep.tile([P, BLOCKS, E * C], F32, name="gate_sb")
+        for kind, first, count in LOADS:
+            if kind == "x":
+                for q in range(first, first + count):
+                    planes[q] = keep.tile([P, T], F32, name="plane%d" % q)
+                    nc.sync.dma_start(planes[q][:], x_view[q // PACK, :, q % PACK, :])
+            elif kind == "w":
+                raw = keep.tile([P, count, PACK, N], F32, name="w_raw%d" % first)
+                e, g = first // PASSES, first % PASSES
+                nc.sync.dma_start(raw[:], w_view[e, :, g:g + count])
+                for i in range(count):
+                    w_raw[first + i] = raw[:, i]
+            else:
+                nc.sync.dma_start(gate_sb[:], gate.rearrange("(h p) j -> p h j", p=P))
+
+        windows = []
+        for nb in range(BLOCKS):
+            window = keep.tile([P, T], F32, name="window%d" % nb)
+            nc.vector.memset(window[:], 0.0)
+            windows.append(window)
+
+        g4 = {}
+        xg = {}
+        x_codes = {}
+        x_scales = {}
+
+        def interleave(engine, dst, src):
+            d = dst
+            s = src.rearrange("p t n -> p n t")
+            if engine == "vector":
+                nc.vector.tensor_copy(out=d, in_=s)
+            else:
+                nc.scalar.copy(out=d, in_=s)
+
+        def gather(g, t, h):
+            if t == 0:
+                g4[(g, h)] = g4_pool.tile([P, PACK, HALF], F32, name="g4")
+            nc.vector.tensor_copy(
+                g4[(g, h)][:, t, :],
+                planes[g * PACK + t][:].indirect(offsets[:, h * (HALF // 16):(h + 1) * (HALF // 16)]),
+            )
+
+        def x_copy(engine, g, h):
+            xg[(g, h)] = xg_pool.tile([P, HALF, PACK], BF16, name="xg", align_bytes=64)
+            interleave(engine, xg[(g, h)][:], g4[(g, h)][:])
+
+        def x_quant(g, h):
+            x_codes[(g, h)] = keep.tile([P, HALF], U32, name="x_codes%d_%d" % (g, h), align_bytes=64)
+            x_scales[(g, h)] = keep.tile([P, HALF], U8, name="x_scales%d_%d" % (g, h), align_bytes=64)
+            nc.vector.quantize_mx(
+                out=x_codes[(g, h)][:].bitcast(FP8X4),
+                scales=x_scales[(g, h)][:],
+                in_=xg[(g, h)][:].rearrange("p n t -> p (n t)"),
+            )
+
+        wg = {}
+        w_codes = {}
+        w_scales = {}
+        acc = {}
+
+        def w_copy(engine, c, lo, hi):
+            if lo == 0:
+                wg[c] = wg_pool.tile([P, N, PACK], BF16, name="wg", align_bytes=64)
+                w_codes[c] = keep.tile([P, N], U32, name="w_codes%d" % c, align_bytes=64)
+                w_scales[c] = keep.tile([P, N], U8, name="w_scales%d" % c, align_bytes=64)
+            interleave(engine, wg[c][:, lo:hi, :], w_raw[c][:, :, lo:hi])
+
+        def w_quant(c, lo, hi):
+            nc.vector.quantize_mx(
+                out=w_codes[c][:, lo:hi].bitcast(FP8X4),
+                scales=w_scales[c][:, lo:hi],
+                in_=wg[c][:, lo:hi, :].rearrange("p n j -> p (n j)"),
+            )
+
+        def multiply(c, nb):
+            e, g = c // PASSES, c % PASSES
+            h, lo = (e * C) // HALF, (e * C) % HALF
+            if g == 0:
+                acc[(e, nb)] = psum.tile([P, C], F32, name="acc%d_%d" % (e, nb))
+            nc.tensor.matmul_mx(
+                out=acc[(e, nb)][:],
+                lhsT=w_codes[c][:, nb * P:(nb + 1) * P].bitcast(FP8X4),
+                lhsT_scale=w_scales[c][:, nb * P:(nb + 1) * P],
+                rhs=x_codes[(g, h)][:, lo:lo + C].bitcast(FP8X4),
+                rhs_scale=x_scales[(g, h)][:, lo:lo + C],
+                start=(g == 0),
+                stop=(g == PASSES - 1),
+            )
+
+        def finish(e):
+            ys = []
+            for nb in range(BLOCKS):
+                y = keep.tile([P, C], F32, name="y%d_%d" % (e, nb))
+                nc.scalar.activation(out=y[:], in_=acc[(e, nb)][:], func=RELU, bias=bias[:, nb, e:e + 1])
+                ys.append(y)
+            for nb in range(BLOCKS):
+                nc.vector.tensor_tensor(
+                    windows[nb][:].indirect(offsets[:, e * (C // 16):(e + 1) * (C // 16)]),
+                    ys[nb][:],
+                    gate_sb[:, nb, e * C:(e + 1) * C],
+                    MULT,
+                )
+
+        def whole(c):
+            w_quant(c, 0, N)
+            for nb in range(BLOCKS):
+                multiply(c, nb)
+
+        last = PASSES - 1
+        for g in range(PASSES):
+            for t in range(PACK):
+                for h in range(HALVES):
+                    gather(g, t, h)
+                if g > 0 and t in (1, 2):
+                    x_quant(g - 1, t - 1)
+            if g < last:
+                for h in range(HALVES):
+                    x_copy("scalar", g, h)
+                if g < EARLY:
+                    w_copy("scalar", g, 0, N)
+        for h in range(HALVES):
+            x_copy("vector", last, h)
+        for h in range(HALVES):
+            w_quant(h, 0, N)
+            x_quant(last, h)
+        w_quant(2, 0, N)
+        for c in range(EARLY):
+            for nb in range(BLOCKS):
+                multiply(c, nb)
+
+        for c in range(EARLY, CHUNKS - 1):
+            w_copy("vector" if c in W_ON_VECTOR else "scalar", c, 0, N)
+            if c > EARLY:
+                whole(c - 1)
+            if c >= 5 and c % PASSES == 1:
+                finish(c // PASSES - 1)
+        c = CHUNKS - 1
+        w_copy("vector", c, 0, P)
+        w_copy("scalar", c, P, N)
+        whole(c - 1)
+        for nb in range(BLOCKS):
+            w_quant(c, nb * P, (nb + 1) * P)
+            multiply(c, nb)
+        finish(E - 1)
+
+        out_view = out.rearrange("(h p) t -> h p t", p=P)
+        for nb in range(BLOCKS):
+            nc.sync.dma_start(out_view[nb], windows[nb][:])

@@ -76,8 +76,8 @@ def tile_routed_moe_kernel(tc, xT, w, b, gate, offs, out):
         x_scales = {}
 
         def interleave(engine, dst, src):
-            d = dst
-            s = src.rearrange("p t n -> p n t")
+            d = dst.rearrange("p (c i) t -> p c t i", i=4)
+            s = src.rearrange("p t (c i) -> p c t i", i=4)
             if engine == "vector":
                 nc.vector.tensor_copy(out=d, in_=s)
             else:

@@ -11,6 +11,8 @@ U32 = mybir.dt.uint32
 U16 = mybir.dt.uint16
 U8 = mybir.dt.uint8
 FP8X4 = mybir.dt.float8_e4m3fn_x4
+ADD = mybir.AluOpType.add
+MAX = mybir.AluOpType.max
 MULT = mybir.AluOpType.mult
 RELU = mybir.ActivationFunctionType.Relu
 
@@ -22,12 +24,14 @@ HALF = 256
 HALVES = E * C // HALF
 BLOCKS = N // P
 
-W_ON_VECTOR = (6, 10, 14)
-EARLY = 3
+W_ON_VECTOR = (7, 11)
+EARLY = {}
+X_LAST = ("vector", "vector")
+QUANT_LAG = 1
+FINISH_LAG = 1
 LOADS = (
-    ("x", 0, 5), ("w", 0, 1), ("x", 5, 4), ("w", 1, 1), ("x", 9, 5), ("w", 2, 1), ("x", 14, 2),
-    ("w", 3, 1), ("w", 4, 2), ("gate", 0, 0), ("w", 6, 2), ("w", 8, 2), ("w", 10, 2), ("w", 12, 2),
-    ("w", 14, 1), ("w", 15, 1),
+    ("x", 0, 16), ("w", 0, 2), ("w", 2, 2), ("w", 4, 2), ("gate", 0, 0), ("w", 6, 2), ("w", 8, 2), ("w", 10, 2),
+    ("w", 12, 2), ("w", 14, 1), ("w", 15, 1),
 )
 
 
@@ -142,7 +146,12 @@ def tile_routed_moe_kernel(tc, xT, w, b, gate, offs, out):
             ys = []
             for nb in range(BLOCKS):
                 y = keep.tile([P, C], F32, name="y%d_%d" % (e, nb))
-                nc.scalar.activation(out=y[:], in_=acc[(e, nb)][:], func=RELU, bias=bias[:, nb, e:e + 1])
+                if e < E - 1:
+                    nc.vector.tensor_scalar(
+                        out=y[:], in0=acc[(e, nb)][:], scalar1=bias[:, nb, e:e + 1], scalar2=0.0, op0=ADD, op1=MAX
+                    )
+                else:
+                    nc.scalar.activation(out=y[:], in_=acc[(e, nb)][:], func=RELU, bias=bias[:, nb, e:e + 1])
                 ys.append(y)
             for nb in range(BLOCKS):
                 nc.vector.tensor_tensor(
@@ -167,28 +176,40 @@ def tile_routed_moe_kernel(tc, xT, w, b, gate, offs, out):
             if g < last:
                 for h in range(HALVES):
                     x_copy("scalar", g, h)
-                if g < EARLY:
-                    w_copy("scalar", g, 0, N)
+                if g in EARLY:
+                    w_copy("scalar", EARLY[g], 0, N)
         for h in range(HALVES):
-            x_copy("vector", last, h)
+            x_copy(X_LAST[h], last, h)
+        n_early = len(EARLY)
         for h in range(HALVES):
-            w_quant(h, 0, N)
+            if h < n_early:
+                w_quant(h, 0, N)
             x_quant(last, h)
-        w_quant(2, 0, N)
-        for c in range(EARLY):
+        for c in range(HALVES, n_early):
+            w_quant(c, 0, N)
+        for c in range(n_early):
             for nb in range(BLOCKS):
                 multiply(c, nb)
 
-        for c in range(EARLY, CHUNKS - 1):
+        quantised = n_early - 1
+        finished = -1
+        for c in range(n_early, CHUNKS - 1):
             w_copy("vector" if c in W_ON_VECTOR else "scalar", c, 0, N)
-            if c > EARLY:
-                whole(c - 1)
-            if c >= 5 and c % PASSES == 1:
-                finish(c // PASSES - 1)
+            while quantised < c - QUANT_LAG:
+                quantised += 1
+                whole(quantised)
+            while finished < E - 2 and PASSES * (finished + 1) + PASSES - 1 + FINISH_LAG <= quantised:
+                finished += 1
+                finish(finished)
         c = CHUNKS - 1
         w_copy("vector", c, 0, P)
         w_copy("scalar", c, P, N)
-        whole(c - 1)
+        while quantised < c - 1:
+            quantised += 1
+            whole(quantised)
+        while finished < E - 2:
+            finished += 1
+            finish(finished)
         for nb in range(BLOCKS):
             w_quant(c, nb * P, (nb + 1) * P)
             multiply(c, nb)

@@ -24,14 +24,14 @@ HALF = 256
 HALVES = E * C // HALF
 BLOCKS = N // P
 
-W_ON_VECTOR = (7, 11)
+W_ON_VECTOR = (7, 9, 11)
 EARLY = {}
 X_LAST = ("vector", "vector")
 QUANT_LAG = 1
-FINISH_LAG = 1
+FINISH_LAG = 0
 LOADS = (
-    ("x", 0, 16), ("w", 0, 2), ("w", 2, 2), ("w", 4, 2), ("gate", 0, 0), ("w", 6, 2), ("w", 8, 2), ("w", 10, 2),
-    ("w", 12, 2), ("w", 14, 1), ("w", 15, 1),
+    ("x", 0, 16), ("b", 0, 0), ("w", 0, 2), ("w", 2, 2), ("w", 4, 2), ("gate", 0, 0), ("w", 6, 2), ("w", 8, 2),
+    ("w", 10, 2), ("w", 12, 1), ("w", 13, 1), ("w", 14, 1), ("w", 15, 1),
 )
 
 
@@ -47,7 +47,6 @@ def tile_routed_moe_kernel(tc, xT, w, b, gate, offs, out):
         offsets = keep.tile([P, E * C // 16], U16, name="offsets")
         nc.sync.dma_start(offsets[:], offs)
         bias = keep.tile([P, BLOCKS, E], F32, name="bias")
-        nc.sync.dma_start(bias[:], b.rearrange("(h p) e -> p h e", p=P))
 
         x_view = xT.rearrange("(g p t) n -> g p t n", p=P, t=PACK)
         w_view = w.rearrange("e (g p j) n -> e p g j n", p=P, j=PACK)
@@ -65,6 +64,8 @@ def tile_routed_moe_kernel(tc, xT, w, b, gate, offs, out):
                 nc.sync.dma_start(raw[:], w_view[e, :, g:g + count])
                 for i in range(count):
                     w_raw[first + i] = raw[:, i]
+            elif kind == "b":
+                nc.sync.dma_start(bias[:], b.rearrange("(h p) e -> p h e", p=P))
             else:
                 nc.sync.dma_start(gate_sb[:], gate.rearrange("(h p) j -> p h j", p=P))
 

@@ -23,16 +23,9 @@ CHUNKS = E * PASSES
 HALF = 256
 HALVES = E * C // HALF
 BLOCKS = N // P
+LINE = 4
 
 W_ON_VECTOR = (7, 9, 11)
-EARLY = {}
-X_LAST = ("vector", "vector")
-QUANT_LAG = 1
-FINISH_LAG = 0
-LOADS = (
-    ("x", 0, 16), ("b", 0, 0), ("w", 0, 2), ("w", 2, 2), ("w", 4, 2), ("gate", 0, 0), ("w", 6, 2), ("w", 8, 2),
-    ("w", 10, 2), ("w", 12, 1), ("w", 13, 1), ("w", 14, 1), ("w", 15, 1),
-)
 
 
 def tile_routed_moe_kernel(tc, xT, w, b, gate, offs, out):
@@ -47,27 +40,32 @@ def tile_routed_moe_kernel(tc, xT, w, b, gate, offs, out):
         offsets = keep.tile([P, E * C // 16], U16, name="offsets")
         nc.sync.dma_start(offsets[:], offs)
         bias = keep.tile([P, BLOCKS, E], F32, name="bias")
+        gate_sb = keep.tile([P, BLOCKS, E * C], F32, name="gate_sb")
 
         x_view = xT.rearrange("(g p t) n -> g p t n", p=P, t=PACK)
-        w_view = w.rearrange("e (g p j) n -> e p g j n", p=P, j=PACK)
         planes = {}
+        for q in range(PASSES * PACK):
+            planes[q] = keep.tile([P, T], F32, name="plane%d" % q)
+            nc.sync.dma_start(planes[q][:], x_view[q // PACK, :, q % PACK, :])
+        nc.sync.dma_start(bias[:], b.rearrange("(h p) e -> p h e", p=P))
+
+        w_view = w.rearrange("e (g p j) n -> e p g j n", p=P, j=PACK)
         w_raw = {}
-        gate_sb = keep.tile([P, BLOCKS, E * C], F32, name="gate_sb")
-        for kind, first, count in LOADS:
-            if kind == "x":
-                for q in range(first, first + count):
-                    planes[q] = keep.tile([P, T], F32, name="plane%d" % q)
-                    nc.sync.dma_start(planes[q][:], x_view[q // PACK, :, q % PACK, :])
-            elif kind == "w":
-                raw = keep.tile([P, count, PACK, N], F32, name="w_raw%d" % first)
-                e, g = first // PASSES, first % PASSES
-                nc.sync.dma_start(raw[:], w_view[e, :, g:g + count])
-                for i in range(count):
-                    w_raw[first + i] = raw[:, i]
-            elif kind == "b":
-                nc.sync.dma_start(bias[:], b.rearrange("(h p) e -> p h e", p=P))
-            else:
-                nc.sync.dma_start(gate_sb[:], gate.rearrange("(h p) j -> p h j", p=P))
+
+        def load_w(first, count):
+            raw = keep.tile([P, count, PACK, N], F32, name="w_raw%d" % first)
+            e, g = first // PASSES, first % PASSES
+            nc.sync.dma_start(raw[:], w_view[e, :, g:g + count])
+            for i in range(count):
+                w_raw[first + i] = raw[:, i]
+
+        for first in range(0, 6, 2):
+            load_w(first, 2)
+        nc.sync.dma_start(gate_sb[:], gate.rearrange("(h p) j -> p h j", p=P))
+        for first in range(6, CHUNKS - PASSES, 2):
+            load_w(first, 2)
+        for first in range(CHUNKS - PASSES, CHUNKS):
+            load_w(first, 1)
 
         windows = []
         for nb in range(BLOCKS):
@@ -75,18 +73,18 @@ def tile_routed_moe_kernel(tc, xT, w, b, gate, offs, out):
             nc.vector.memset(window[:], 0.0)
             windows.append(window)
 
-        g4 = {}
-        xg = {}
-        x_codes = {}
-        x_scales = {}
-
         def interleave(engine, dst, src):
-            d = dst.rearrange("p (c i) t -> p c t i", i=4)
-            s = src.rearrange("p t (c i) -> p c t i", i=4)
+            d = dst.rearrange("p (c i) t -> p c t i", i=LINE)
+            s = src.rearrange("p t (c i) -> p c t i", i=LINE)
             if engine == "vector":
                 nc.vector.tensor_copy(out=d, in_=s)
             else:
                 nc.scalar.copy(out=d, in_=s)
+
+        g4 = {}
+        xg = {}
+        x_codes = {}
+        x_scales = {}
 
         def gather(g, t, h):
             if t == 0:
@@ -113,9 +111,10 @@ def tile_routed_moe_kernel(tc, xT, w, b, gate, offs, out):
         w_codes = {}
         w_scales = {}
         acc = {}
+        ys = {}
 
         def w_copy(engine, c, lo, hi):
-            if lo == 0:
+            if c not in wg:
                 wg[c] = wg_pool.tile([P, N, PACK], BF16, name="wg", align_bytes=64)
                 w_codes[c] = keep.tile([P, N], U32, name="w_codes%d" % c, align_bytes=64)
                 w_scales[c] = keep.tile([P, N], U8, name="w_scales%d" % c, align_bytes=64)
@@ -143,29 +142,29 @@ def tile_routed_moe_kernel(tc, xT, w, b, gate, offs, out):
                 stop=(g == PASSES - 1),
             )
 
-        def finish(e):
-            ys = []
+        def quant_and_multiply(c):
+            w_quant(c, 0, N)
+            for nb in range(BLOCKS):
+                multiply(c, nb)
+
+        def bias_relu(engine, e):
             for nb in range(BLOCKS):
                 y = keep.tile([P, C], F32, name="y%d_%d" % (e, nb))
-                if e < E - 1:
+                if engine == "vector":
                     nc.vector.tensor_scalar(
                         out=y[:], in0=acc[(e, nb)][:], scalar1=bias[:, nb, e:e + 1], scalar2=0.0, op0=ADD, op1=MAX
                     )
                 else:
                     nc.scalar.activation(out=y[:], in_=acc[(e, nb)][:], func=RELU, bias=bias[:, nb, e:e + 1])
-                ys.append(y)
-            for nb in range(BLOCKS):
-                nc.vector.tensor_tensor(
-                    windows[nb][:].indirect(offsets[:, e * (C // 16):(e + 1) * (C // 16)]),
-                    ys[nb][:],
-                    gate_sb[:, nb, e * C:(e + 1) * C],
-                    MULT,
-                )
+                ys[(e, nb)] = y
 
-        def whole(c):
-            w_quant(c, 0, N)
-            for nb in range(BLOCKS):
-                multiply(c, nb)
+        def way_back(e, nb):
+            nc.vector.tensor_tensor(
+                windows[nb][:].indirect(offsets[:, e * (C // 16):(e + 1) * (C // 16)]),
+                ys[(e, nb)][:],
+                gate_sb[:, nb, e * C:(e + 1) * C],
+                MULT,
+            )
 
         last = PASSES - 1
         for g in range(PASSES):
@@ -177,44 +176,37 @@ def tile_routed_moe_kernel(tc, xT, w, b, gate, offs, out):
             if g < last:
                 for h in range(HALVES):
                     x_copy("scalar", g, h)
-                if g in EARLY:
-                    w_copy("scalar", EARLY[g], 0, N)
         for h in range(HALVES):
-            x_copy(X_LAST[h], last, h)
-        n_early = len(EARLY)
+            x_copy("vector", last, h)
         for h in range(HALVES):
-            if h < n_early:
-                w_quant(h, 0, N)
             x_quant(last, h)
-        for c in range(HALVES, n_early):
-            w_quant(c, 0, N)
-        for c in range(n_early):
-            for nb in range(BLOCKS):
-                multiply(c, nb)
 
-        quantised = n_early - 1
-        finished = -1
-        for c in range(n_early, CHUNKS - 1):
+        for c in range(CHUNKS - PASSES + 1):
             w_copy("vector" if c in W_ON_VECTOR else "scalar", c, 0, N)
-            while quantised < c - QUANT_LAG:
-                quantised += 1
-                whole(quantised)
-            while finished < E - 2 and PASSES * (finished + 1) + PASSES - 1 + FINISH_LAG <= quantised:
-                finished += 1
-                finish(finished)
-        c = CHUNKS - 1
-        w_copy("vector", c, 0, P)
-        w_copy("scalar", c, P, N)
-        while quantised < c - 1:
-            quantised += 1
-            whole(quantised)
-        while finished < E - 2:
-            finished += 1
-            finish(finished)
+            if c > 0:
+                quant_and_multiply(c - 1)
+                if c % PASSES == 0 and c < CHUNKS - PASSES:
+                    bias_relu("vector", c // PASSES - 1)
+                    for nb in range(BLOCKS):
+                        way_back(c // PASSES - 1, nb)
+
+        final = CHUNKS - 1
+        for c in range(CHUNKS - PASSES + 1, final):
+            w_copy("scalar", c, 0, N)
+        w_copy("scalar", final, P, N)
+        bias_relu("vector", E - 2)
+        quant_and_multiply(final - 3)
+        way_back(E - 2, 0)
+        quant_and_multiply(final - 2)
+        w_copy("vector", final, 0, P)
+        quant_and_multiply(final - 1)
         for nb in range(BLOCKS):
-            w_quant(c, nb * P, (nb + 1) * P)
-            multiply(c, nb)
-        finish(E - 1)
+            w_quant(final, nb * P, (nb + 1) * P)
+            multiply(final, nb)
+        way_back(E - 2, 1)
+        bias_relu("scalar", E - 1)
+        for nb in range(BLOCKS):
+            way_back(E - 1, nb)
 
         out_view = out.rearrange("(h p) t -> h p t", p=P)
         for nb in range(BLOCKS):

@@ -25,7 +25,12 @@ HALVES = E * C // HALF
 BLOCKS = N // P
 LINE = 4
 
-W_ON_VECTOR = (7, 9, 11)
+W_ON_VECTOR = (11,)
+X_LAST = "vector"
+EARLY = ()
+W_LOADS = ((0, 2), (2, 2), (4, 2), "gate", (6, 2), (8, 2), (10, 2), (12, 1), (13, 1), (14, 1), (15, 1))
+PLANE_LOADS = (1, 1, 1, 1, 1, 1, 2, 1, 1, 2, 1, 1, 2)
+GATE_LATE = True
 
 
 def tile_routed_moe_kernel(tc, xT, w, b, gate, offs, out):
@@ -40,14 +45,9 @@ def tile_routed_moe_kernel(tc, xT, w, b, gate, offs, out):
         offsets = keep.tile([P, E * C // 16], U16, name="offsets")
         nc.sync.dma_start(offsets[:], offs)
         bias = keep.tile([P, BLOCKS, E], F32, name="bias")
-        gate_sb = keep.tile([P, BLOCKS, E * C], F32, name="gate_sb")
-
-        x_view = xT.rearrange("(g p t) n -> g p t n", p=P, t=PACK)
-        planes = {}
-        for q in range(PASSES * PACK):
-            planes[q] = keep.tile([P, T], F32, name="plane%d" % q)
-            nc.sync.dma_start(planes[q][:], x_view[q // PACK, :, q % PACK, :])
-        nc.sync.dma_start(bias[:], b.rearrange("(h p) e -> p h e", p=P))
+        early_slots = (E - 1) * C if GATE_LATE else E * C
+        gate_a = keep.tile([P, BLOCKS, early_slots], F32, name="gate_a")
+        gate_view = gate.rearrange("(h p) j -> p h j", p=P)
 
         w_view = w.rearrange("e (g p j) n -> e p g j n", p=P, j=PACK)
         w_raw = {}
@@ -59,13 +59,29 @@ def tile_routed_moe_kernel(tc, xT, w, b, gate, offs, out):
             for i in range(count):
                 w_raw[first + i] = raw[:, i]
 
-        for first in range(0, 6, 2):
-            load_w(first, 2)
-        nc.sync.dma_start(gate_sb[:], gate.rearrange("(h p) j -> p h j", p=P))
-        for first in range(6, CHUNKS - PASSES, 2):
-            load_w(first, 2)
-        for first in range(CHUNKS - PASSES, CHUNKS):
-            load_w(first, 1)
+        x_view = xT.rearrange("(g p t) n -> g p t n", p=P, t=PACK)
+        early_after = dict(EARLY)
+        planes = {}
+        q = 0
+        for count in PLANE_LOADS:
+            group = keep.tile([P, count, T], F32, name="planes%d" % q)
+            nc.sync.dma_start(group[:], x_view[q // PACK, :, q % PACK:q % PACK + count, :])
+            for i in range(count):
+                planes[q + i] = group[:, i, :]
+            q += count
+            if q - 1 in early_after:
+                load_w(early_after[q - 1], 1)
+        nc.sync.dma_start(bias[:], b.rearrange("(h p) e -> p h e", p=P))
+
+        for item in W_LOADS:
+            if item == "gate":
+                nc.sync.dma_start(gate_a[:], gate_view[:, :, 0:early_slots])
+            else:
+                load_w(item[0], item[1])
+        gate_b = None
+        if GATE_LATE:
+            gate_b = keep.tile([P, BLOCKS, C], F32, name="gate_b")
+            nc.sync.dma_start(gate_b[:], gate_view[:, :, early_slots:E * C])
 
         windows = []
         for nb in range(BLOCKS):
@@ -91,7 +107,7 @@ def tile_routed_moe_kernel(tc, xT, w, b, gate, offs, out):
                 g4[(g, h)] = g4_pool.tile([P, PACK, HALF], F32, name="g4")
             nc.vector.tensor_copy(
                 g4[(g, h)][:, t, :],
-                planes[g * PACK + t][:].indirect(offsets[:, h * (HALF // 16):(h + 1) * (HALF // 16)]),
+                planes[g * PACK + t].indirect(offsets[:, h * (HALF // 16):(h + 1) * (HALF // 16)]),
             )
 
         def x_copy(engine, g, h):
@@ -162,9 +178,22 @@ def tile_routed_moe_kernel(tc, xT, w, b, gate, offs, out):
             nc.vector.tensor_tensor(
                 windows[nb][:].indirect(offsets[:, e * (C // 16):(e + 1) * (C // 16)]),
                 ys[(e, nb)][:],
-                gate_sb[:, nb, e * C:(e + 1) * C],
+                gate_b[:, nb, :] if (GATE_LATE and e == E - 1) else gate_a[:, nb, e * C:(e + 1) * C],
                 MULT,
             )
+
+        copied = set()
+        quantised = set()
+
+        def do_copy(c):
+            if c not in copied:
+                w_copy("vector" if c in W_ON_VECTOR else "scalar", c, 0, N)
+                copied.add(c)
+
+        def do_quant(c):
+            if c not in quantised:
+                quant_and_multiply(c)
+                quantised.add(c)
 
         last = PASSES - 1
         for g in range(PASSES):
@@ -173,18 +202,23 @@ def tile_routed_moe_kernel(tc, xT, w, b, gate, offs, out):
                     gather(g, t, h)
                 if g > 0 and t in (1, 2):
                     x_quant(g - 1, t - 1)
+                q = g * PACK + t
+                if q - 1 in early_after:
+                    do_copy(early_after[q - 1])
+                if q - 3 in early_after:
+                    do_quant(early_after[q - 3])
             if g < last:
                 for h in range(HALVES):
                     x_copy("scalar", g, h)
         for h in range(HALVES):
-            x_copy("vector", last, h)
+            x_copy(X_LAST, last, h)
         for h in range(HALVES):
             x_quant(last, h)
 
         for c in range(CHUNKS - PASSES + 1):
-            w_copy("vector" if c in W_ON_VECTOR else "scalar", c, 0, N)
+            do_copy(c)
             if c > 0:
-                quant_and_multiply(c - 1)
+                do_quant(c - 1)
                 if c % PASSES == 0 and c < CHUNKS - PASSES:
                     bias_relu("vector", c // PASSES - 1)
                     for nb in range(BLOCKS):

@@ -28,7 +28,7 @@ LINE = 4
 W_ON_VECTOR = (11,)
 X_LAST = "vector"
 EARLY = ()
-W_LOADS = ((0, 2), (2, 2), (4, 2), "gate", (6, 2), (8, 2), (10, 2), (12, 1), (13, 1), (14, 1), (15, 1))
+W_LOADS = ((0, 1), (1, 1), (2, 1), (3, 1), (4, 1), (5, 1), "gate", (6, 1), (7, 1), (8, 1), (9, 1), (10, 1), (11, 1), (12, 1), (13, 1), (14, 1), (15, 1))
 PLANE_LOADS = (1, 1, 1, 1, 1, 1, 2, 1, 1, 2, 1, 1, 2)
 GATE_LATE = True
 

@@ -44,7 +44,7 @@ def tile_routed_moe_kernel(tc, xT, w, b, gate, offs, out):
 
         offsets = keep.tile([P, E * C // 16], U16, name="offsets")
         nc.sync.dma_start(offsets[:], offs)
-        bias = keep.tile([P, BLOCKS, E], F32, name="bias")
+        bias = keep.tile([P, BLOCKS, 2 * E], F32, name="bias")
         early_slots = (E - 1) * C if GATE_LATE else E * C
         gate_a = keep.tile([P, BLOCKS, early_slots], F32, name="gate_a")
         gate_view = gate.rearrange("(h p) j -> p h j", p=P)
@@ -71,7 +71,7 @@ def tile_routed_moe_kernel(tc, xT, w, b, gate, offs, out):
             q += count
             if q - 1 in early_after:
                 load_w(early_after[q - 1], 1)
-        nc.sync.dma_start(bias[:], b.rearrange("(h p) e -> p h e", p=P))
+        nc.sync.dma_start(bias[:, :, 0:E], b.rearrange("(h p) e -> p h e", p=P))
 
         for item in W_LOADS:
             if item == "gate":

from contextlib import ExitStack

import concourse.mybir as mybir

K, T, E, C, N = 2048, 1024, 4, 128, 256
FLOPS = 2 * K * N * E * C

F32 = mybir.dt.float32
BF16 = mybir.dt.bfloat16
U32 = mybir.dt.uint32
U16 = mybir.dt.uint16
U8 = mybir.dt.uint8
FP8X4 = mybir.dt.float8_e4m3fn_x4
ADD = mybir.AluOpType.add
MAX = mybir.AluOpType.max
MULT = mybir.AluOpType.mult
RELU = mybir.ActivationFunctionType.Relu

P = 128
PACK = 4
PASSES = K // (P * PACK)
CHUNKS = E * PASSES
HALF = 256
HALVES = E * C // HALF
BLOCKS = N // P
LINE = 4

W_ON_VECTOR = (11,)
X_LAST = "vector"
EARLY = ()
W_LOADS = ((0, 1), (1, 1), (2, 1), (3, 1), (4, 1), (5, 1), "gate", (6, 1), (7, 1), (8, 1), (9, 1), (10, 1), (11, 1), (12, 1), (13, 1), (14, 1), (15, 1))
PLANE_LOADS = (1, 1, 1, 1, 1, 1, 2, 1, 1, 2, 1, 1, 2)
GATE_LATE = True


def tile_routed_moe_kernel(tc, xT, w, b, gate, offs, out):
    nc = tc.nc
    with ExitStack() as ctx:
        keep = ctx.enter_context(tc.tile_pool(name="keep", bufs=1))
        g4_pool = ctx.enter_context(tc.tile_pool(name="g4_pool", bufs=4))
        xg_pool = ctx.enter_context(tc.tile_pool(name="xg_pool", bufs=4))
        wg_pool = ctx.enter_context(tc.tile_pool(name="wg_pool", bufs=6))
        psum = ctx.enter_context(tc.psum_pool(name="psum", bufs=1))

        offsets = keep.tile([P, E * C // 16], U16, name="offsets")
        nc.sync.dma_start(offsets[:], offs)
        bias = keep.tile([P, BLOCKS, 2 * E], F32, name="bias")
        early_slots = (E - 1) * C if GATE_LATE else E * C
        gate_a = keep.tile([P, BLOCKS, early_slots], F32, name="gate_a")
        gate_view = gate.rearrange("(h p) j -> p h j", p=P)

        w_view = w.rearrange("e (g p j) n -> e p g j n", p=P, j=PACK)
        w_raw = {}

        def load_w(first, count):
            raw = keep.tile([P, count, PACK, N], F32, name="w_raw%d" % first)
            e, g = first // PASSES, first % PASSES
            nc.sync.dma_start(raw[:], w_view[e, :, g:g + count])
            for i in range(count):
                w_raw[first + i] = raw[:, i]

        x_view = xT.rearrange("(g p t) n -> g p t n", p=P, t=PACK)
        early_after = dict(EARLY)
        planes = {}
        q = 0
        for count in PLANE_LOADS:
            group = keep.tile([P, count, T], F32, name="planes%d" % q)
            nc.sync.dma_start(group[:], x_view[q // PACK, :, q % PACK:q % PACK + count, :])
            for i in range(count):
                planes[q + i] = group[:, i, :]
            q += count
            if q - 1 in early_after:
                load_w(early_after[q - 1], 1)
        nc.sync.dma_start(bias[:, :, 0:E], b.rearrange("(h p) e -> p h e", p=P))

        for item in W_LOADS:
            if item == "gate":
                nc.sync.dma_start(gate_a[:], gate_view[:, :, 0:early_slots])
            else:
                load_w(item[0], item[1])
        gate_b = None
        if GATE_LATE:
            gate_b = keep.tile([P, BLOCKS, C], F32, name="gate_b")
            nc.sync.dma_start(gate_b[:], gate_view[:, :, early_slots:E * C])

        windows = []
        for nb in range(BLOCKS):
            window = keep.tile([P, T], F32, name="window%d" % nb)
            nc.vector.memset(window[:], 0.0)
            windows.append(window)

        def interleave(engine, dst, src):
            d = dst.rearrange("p (c i) t -> p c t i", i=LINE)
            s = src.rearrange("p t (c i) -> p c t i", i=LINE)
            if engine == "vector":
                nc.vector.tensor_copy(out=d, in_=s)
            else:
                nc.scalar.copy(out=d, in_=s)

        g4 = {}
        xg = {}
        x_codes = {}
        x_scales = {}

        def gather(g, t, h):
            if t == 0:
                g4[(g, h)] = g4_pool.tile([P, PACK, HALF], F32, name="g4")
            nc.vector.tensor_copy(
                g4[(g, h)][:, t, :],
                planes[g * PACK + t].indirect(offsets[:, h * (HALF // 16):(h + 1) * (HALF // 16)]),
            )

        def x_copy(engine, g, h):
            xg[(g, h)] = xg_pool.tile([P, HALF, PACK], BF16, name="xg", align_bytes=64)
            interleave(engine, xg[(g, h)][:], g4[(g, h)][:])

        def x_quant(g, h):
            x_codes[(g, h)] = keep.tile([P, HALF], U32, name="x_codes%d_%d" % (g, h), align_bytes=64)
            x_scales[(g, h)] = keep.tile([P, HALF], U8, name="x_scales%d_%d" % (g, h), align_bytes=64)
            nc.vector.quantize_mx(
                out=x_codes[(g, h)][:].bitcast(FP8X4),
                scales=x_scales[(g, h)][:],
                in_=xg[(g, h)][:].rearrange("p n t -> p (n t)"),
            )

        wg = {}
        w_codes = {}
        w_scales = {}
        acc = {}
        ys = {}

        def w_copy(engine, c, lo, hi):
            if c not in wg:
                wg[c] = wg_pool.tile([P, N, PACK], BF16, name="wg", align_bytes=64)
                w_codes[c] = keep.tile([P, N], U32, name="w_codes%d" % c, align_bytes=64)
                w_scales[c] = keep.tile([P, N], U8, name="w_scales%d" % c, align_bytes=64)
            interleave(engine, wg[c][:, lo:hi, :], w_raw[c][:, :, lo:hi])

        def w_quant(c, lo, hi):
            nc.vector.quantize_mx(
                out=w_codes[c][:, lo:hi].bitcast(FP8X4),
                scales=w_scales[c][:, lo:hi],
                in_=wg[c][:, lo:hi, :].rearrange("p n j -> p (n j)"),
            )

        def multiply(c, nb):
            e, g = c // PASSES, c % PASSES
            h, lo = (e * C) // HALF, (e * C) % HALF
            if g == 0:
                acc[(e, nb)] = psum.tile([P, C], F32, name="acc%d_%d" % (e, nb))
            nc.tensor.matmul_mx(
                out=acc[(e, nb)][:],
                lhsT=w_codes[c][:, nb * P:(nb + 1) * P].bitcast(FP8X4),
                lhsT_scale=w_scales[c][:, nb * P:(nb + 1) * P],
                rhs=x_codes[(g, h)][:, lo:lo + C].bitcast(FP8X4),
                rhs_scale=x_scales[(g, h)][:, lo:lo + C],
                start=(g == 0),
                stop=(g == PASSES - 1),
            )

        def quant_and_multiply(c):
            w_quant(c, 0, N)
            for nb in range(BLOCKS):
                multiply(c, nb)

        def bias_relu(engine, e):
            for nb in range(BLOCKS):
                y = keep.tile([P, C], F32, name="y%d_%d" % (e, nb))
                if engine == "vector":
                    nc.vector.tensor_scalar(
                        out=y[:], in0=acc[(e, nb)][:], scalar1=bias[:, nb, e:e + 1], scalar2=0.0, op0=ADD, op1=MAX
                    )
                else:
                    nc.scalar.activation(out=y[:], in_=acc[(e, nb)][:], func=RELU, bias=bias[:, nb, e:e + 1])
                ys[(e, nb)] = y

        def way_back(e, nb):
            nc.vector.tensor_tensor(
                windows[nb][:].indirect(offsets[:, e * (C // 16):(e + 1) * (C // 16)]),
                ys[(e, nb)][:],
                gate_b[:, nb, :] if (GATE_LATE and e == E - 1) else gate_a[:, nb, e * C:(e + 1) * C],
                MULT,
            )

        copied = set()
        quantised = set()

        def do_copy(c):
            if c not in copied:
                w_copy("vector" if c in W_ON_VECTOR else "scalar", c, 0, N)
                copied.add(c)

        def do_quant(c):
            if c not in quantised:
                quant_and_multiply(c)
                quantised.add(c)

        last = PASSES - 1
        for g in range(PASSES):
            for t in range(PACK):
                for h in range(HALVES):
                    gather(g, t, h)
                if g > 0 and t in (1, 2):
                    x_quant(g - 1, t - 1)
                q = g * PACK + t
                if q - 1 in early_after:
                    do_copy(early_after[q - 1])
                if q - 3 in early_after:
                    do_quant(early_after[q - 3])
            if g < last:
                for h in range(HALVES):
                    x_copy("scalar", g, h)
        for h in range(HALVES):
            x_copy(X_LAST, last, h)
        for h in range(HALVES):
            x_quant(last, h)

        for c in range(CHUNKS - PASSES + 1):
            do_copy(c)
            if c > 0:
                do_quant(c - 1)
                if c % PASSES == 0 and c < CHUNKS - PASSES:
                    bias_relu("vector", c // PASSES - 1)
                    for nb in range(BLOCKS):
                        way_back(c // PASSES - 1, nb)

        final = CHUNKS - 1
        for c in range(CHUNKS - PASSES + 1, final):
            w_copy("scalar", c, 0, N)
        w_copy("scalar", final, P, N)
        bias_relu("vector", E - 2)
        quant_and_multiply(final - 3)
        way_back(E - 2, 0)
        quant_and_multiply(final - 2)
        w_copy("vector", final, 0, P)
        quant_and_multiply(final - 1)
        for nb in range(BLOCKS):
            w_quant(final, nb * P, (nb + 1) * P)
            multiply(final, nb)
        way_back(E - 2, 1)
        bias_relu("scalar", E - 1)
        for nb in range(BLOCKS):
            way_back(E - 1, nb)

        out_view = out.rearrange("(h p) t -> h p t", p=P)
        for nb in range(BLOCKS):
            nc.sync.dma_start(out_view[nb], windows[nb][:])
